import numpy as np
import ml_dtypes


def mxq(x, axis, fmt="e4m3"):
    dtype, down = {"e4m3": (ml_dtypes.float8_e4m3fn, 7), "e5m2": (ml_dtypes.float8_e5m2, 14)}[fmt]
    v = np.moveaxis(np.asarray(x, np.float32).astype(ml_dtypes.bfloat16).astype(np.float64), axis, -1)
    blocks = v.reshape(v.shape[:-1] + (-1, 32))
    amax = np.abs(blocks).max(-1, keepdims=True)
    byte = np.maximum(np.where(amax > 0, np.frexp(amax)[1] - 1 + 127, 0) - down, 1)
    scale = np.exp2(byte - 127.0)
    codes = (blocks / scale).astype(np.float32).astype(dtype).astype(np.float64)
    return np.moveaxis((codes * scale).reshape(v.shape), -1, axis)


WIDE = False


def mx_kscale(k):
    if not WIDE:
        return np.ones(k)
    levels = np.array([30, -30])
    if k % 512:
        return np.exp2(np.random.permutation(np.resize(levels, k // 32))).repeat(32)
    a = np.empty((k // 512, 16))
    for p in range(k // 512):
        a[p, :8] = np.random.permutation(np.resize(levels, 8))
        for g in range(8):
            far = levels[np.abs(levels - a[p, g]) >= 10]
            a[p, g + 8] = far[np.random.randint(len(far))]
    return np.exp2(a.ravel()).repeat(32)


def f64(x):
    return np.asarray(x).astype(np.float64)


def striped(idx):
    return np.tile(np.asarray(idx).reshape(-1, 16).T, (8, 1)).astype(np.uint16)


def unstriped(offs):
    return offs[:16].T.reshape(-1).astype(np.int64)


E2M1 = np.array([0.0, 0.5, 1.0, 1.5, 2.0, 3.0, 4.0, 6.0, -0.0, -0.5, -1.0, -1.5, -2.0, -3.0, -4.0, -6.0])


def pack_weight(w, fmt):
    k, n = w.shape
    w = f64(np.asarray(w, np.float32).astype(ml_dtypes.bfloat16)).reshape(k // 32, 32, n)
    amax = np.abs(w).max(1)
    if fmt in ("e4m3", "e5m2"):
        byte = np.frexp(amax)[1] - 1 + 127 - (7 if fmt == "e4m3" else 14)
    else:
        mant, ex = np.frexp(amax / 6.0)
        byte = np.where(mant > 0.5, ex, ex - 1) + 127
    byte = np.clip(np.where(amax > 0, byte, 1), 1, 254)
    scaled = (w * np.exp2(127.0 - byte)[:, None, :]).reshape(k, n).astype(np.float32)
    by_word = np.ascontiguousarray(scaled.reshape(k // 512, 128, 4, n).transpose(0, 1, 3, 2))
    if fmt in ("e4m3", "e5m2"):
        words = by_word.astype(ml_dtypes.float8_e4m3fn if fmt == "e4m3" else ml_dtypes.float8_e5m2).view(np.uint8)
    else:
        c = by_word.astype(ml_dtypes.float4_e2m1fn).view(np.uint8) & 0xF
        words = (c[..., 0::2] | (c[..., 1::2] << 4)).reshape(k // 512, 128, 2 * n)
    return np.ascontiguousarray(words), np.ascontiguousarray(byte.astype(np.uint8).reshape(k // 512, 16, n))


def unpack_weight(words, scales, fmt):
    g, _, n = scales.shape
    words = np.ascontiguousarray(words).reshape(g, 128, n, -1)
    if fmt in ("e4m3", "e5m2"):
        vals = words.view(ml_dtypes.float8_e4m3fn if fmt == "e4m3" else ml_dtypes.float8_e5m2).astype(np.float64)
    else:
        nib = np.empty((g, 128, n, 4), np.uint8)
        nib[..., 0::2] = words & 0xF
        nib[..., 1::2] = words >> 4
        vals = E2M1[nib]
    vals = vals * np.repeat(np.exp2(scales.astype(np.float64) - 127.0), 8, axis=1)[..., None]
    return vals.transpose(0, 1, 3, 2).reshape(g * 512, n)


K, T, J, R, F, Z, N = 512, 512, 256, 512, 512, 1024, 256


def setup_inputs():
    n = np.random.standard_normal
    idx = np.random.permutation(T)[:J]
    idx2 = np.random.permutation(Z)[:J]
    fk = mx_kscale(K)
    fr = mx_kscale(R)
    ff = mx_kscale(F)
    wp = pack_weight(n((K, R)) * 1 / np.sqrt(K) * fk[:, None] * fr, "e5m2")
    xop = pack_weight(n((F, Z)) / ff[:, None], "e4m3")
    w2p = pack_weight(n((F, R)) * 1 / np.sqrt(F) * ff[:, None] * fr, "e5m2")
    wbp = pack_weight(n((R, N)) * 1 / np.sqrt(R) / fr[:, None], "e4m3")
    return {
        "xf": (n((K, T))).astype(np.float32),
        "ow": (n((K, J)) * 0.7).astype(np.float32),
        "fk": (np.random.uniform(0.5, 2.0, (K, 1)) / fk[:, None]).astype(np.float32),
        "w_words": wp[0],
        "w_scales": wp[1],
        "xo_words": xop[0],
        "xo_scales": xop[1],
        "w2_words": w2p[0],
        "w2_scales": w2p[1],
        "wb_words": wbp[0],
        "wb_scales": wbp[1],
        "rs": (1.0 * n((J, N))).astype(np.float32),
        "offs": striped(idx),
        "offs2": striped(idx2),
    }


def reference(xf, ow, fk, w_words, w_scales, xo_words, xo_scales, w2_words, w2_scales, wb_words, wb_scales, rs, offs, offs2):
    idx = unstriped(offs)
    idx2 = unstriped(offs2)
    wu = unpack_weight(w_words, w_scales, "e5m2")
    xou = unpack_weight(xo_words, xo_scales, "e4m3")
    w2u = unpack_weight(w2_words, w2_scales, "e5m2")
    wbu = unpack_weight(wb_words, wb_scales, "e4m3")
    u = (f64(xf)[:, idx] - f64(ow)) * f64(fk)
    uq = mxq(u, 0, "e5m2")
    xoidx2g = xou[:, idx2]
    a = wu.T @ uq + w2u.T @ xoidx2g
    ha = np.maximum(a, 0.0)
    h1 = np.pad(ha, ((0, 0), (2, 0)))[:, :J]
    hid = ha - 0.5 * h1
    hidq = mxq(hid, 0, "e5m2")
    p = hidq.T @ wbu
    pk2 = np.max(np.abs(p), axis=1, keepdims=True)
    y = p / (pk2 + 0.2) + 0.3 * f64(rs)
    return y

@@ -1,0 +1,197 @@
+from contextlib import ExitStack
+
+import concourse.mybir as mybir
+
+K, T, J, R, F, Z, N = 512, 512, 256, 512, 512, 1024, 256
+FLOPS = 2 * K * R * J + 2 * F * R * J + 2 * R * J * N
+
+F32 = mybir.dt.float32
+BF16 = mybir.dt.bfloat16
+I32 = mybir.dt.int32
+U32 = mybir.dt.uint32
+U16 = mybir.dt.uint16
+U8 = mybir.dt.uint8
+E4M3 = mybir.dt.float8_e4m3fn_x4
+E5M2 = mybir.dt.float8_e5m2_x4
+ALU = mybir.AluOpType
+ACT = mybir.ActivationFunctionType
+
+P = 128
+PACK = 4
+HALF = 128
+LAG = 2
+
+
+def tile_list_sum_offsetpicks_othertable_lagged_rowpeaks_kernel(
+    tc, xf, ow, fk, w_words, w_scales, xo_words, xo_scales, w2_words, w2_scales,
+    wb_words, wb_scales, rs, offs, offs2, out,
+):
+    nc = tc.nc
+    halves = J // HALF
+
+    def words(ap):
+        return ap[0].rearrange("p n t -> p (n t)").bitcast(I32)
+
+    with ExitStack() as ctx:
+        keep = ctx.enter_context(tc.tile_pool(name="keep", bufs=1))
+        psum = ctx.enter_context(tc.psum_pool(name="psum", bufs=1))
+
+        list_x = keep.tile([P, J // 16], U16, name="list_x")
+        list_o = keep.tile([P, J // 16], U16, name="list_o")
+        nc.sync.dma_start(list_o[:], offs2)
+        nc.sync.dma_start(list_x[:], offs)
+
+        fk_sb = keep.tile([P, PACK], F32, name="fk_sb")
+        nc.scalar.dma_start(fk_sb[:], fk.rearrange("(p t) o -> p (t o)", t=PACK))
+        ws_raw = keep.tile([P, 2, R], U8, name="ws_raw", align_bytes=64)
+        xs_raw = keep.tile([P, Z], U8, name="xs_raw", align_bytes=64)
+        planes = keep.tile([P, 2 * R + J + N], U8, name="planes", align_bytes=64)
+        W0, W20, XO0, WB0 = 0, R, 2 * R, 2 * R + J
+        nc.vector.memset(xs_raw[:].bitcast(I32), 0)
+        nc.vector.memset(ws_raw[:].rearrange("p a c -> p (a c)").bitcast(I32), 0)
+        nc.gpsimd.memset(planes[:, WB0 : WB0 + N].bitcast(I32), 0)
+        nc.scalar.dma_start(xs_raw[0:16, :].bitcast(I32), xo_scales[0].bitcast(I32))
+        nc.scalar.dma_start(ws_raw[0:16, 0, :].bitcast(I32), w_scales[0].bitcast(I32))
+        nc.scalar.dma_start(ws_raw[0:16, 1, :].bitcast(I32), w2_scales[0].bitcast(I32))
+        nc.gpsimd.dma_start(planes[0:16, WB0 : WB0 + N].bitcast(I32), wb_scales[0].bitcast(I32))
+
+        lagged = keep.tile([P, (LAG + J) * PACK], F32, name="lagged")
+        before_first = keep.tile([P, LAG * PACK], F32, name="before_first")
+        nc.vector.memset(before_first[:], 0.0)
+        nc.scalar.activation(lagged[:, 0 : LAG * PACK], before_first[:], ACT.Relu, scale=0.5)
+
+        ow_sb = keep.tile([P, PACK, J], F32, name="ow_sb")
+        nc.sync.dma_start(ow_sb[:], ow.rearrange("(p t) j -> p t j", t=PACK))
+        x_rows = xf.rearrange("(p t) c -> p t c", t=PACK)
+        x_sb = []
+        for t in range(PACK):
+            x_t = keep.tile([P, T], F32, name="x_%d" % t)
+            nc.sync.dma_start(x_t[:], x_rows[:, t, :])
+            x_sb.append(x_t)
+        xo_raw = keep.tile([P, Z], I32, name="xo_raw", align_bytes=64)
+        w2_raw = keep.tile([P, R], I32, name="w2_raw", align_bytes=64)
+        w_raw = keep.tile([P, R], I32, name="w_raw", align_bytes=64)
+        nc.sync.dma_start(w_raw[:], words(w_words))
+        nc.sync.dma_start(w2_raw[:], words(w2_words))
+        nc.sync.dma_start(xo_raw[:], words(xo_words))
+
+        xs_g = keep.tile([P, J], U8, name="xs_g", align_bytes=64)
+        nc.vector.tensor_copy(xs_g[:], xs_raw[:].indirect(list_o[:]))
+        for a in range(2):
+            nc.vector.tensor_copy(
+                planes[:, a * R : (a + 1) * R].rearrange("p (t c i) -> p c t i", t=PACK, i=16),
+                ws_raw[:, a, :].rearrange("p (c i t) -> p c t i", t=PACK, i=16),
+            )
+        nc.vector.tensor_copy(planes[:, XO0 : XO0 + J].bitcast(I32), xs_g[:].bitcast(I32))
+        for q in range(1, 4):
+            nc.sync.dma_start(
+                planes[32 * q : 32 * q + 4, :].bitcast(I32), planes[4 * q : 4 * q + 4, :].bitcast(I32)
+            )
+
+        wb_sb = keep.tile([P, N], I32, name="wb_sb", align_bytes=64)
+        nc.sync.dma_start(wb_sb[:], words(wb_words))
+        rs_sb = keep.tile([P, halves, N], F32, name="rs_sb")
+        nc.sync.dma_start(rs_sb[:], rs.rearrange("(h p) n -> p h n", p=P))
+
+        centre = keep.tile([P, PACK, J], F32, name="centre")
+        for t in range(PACK):
+            nc.vector.tensor_scalar(centre[:, t, :], ow_sb[:, t, :], fk_sb[:, t : t + 1], None, ALU.mult)
+        picked = keep.tile([P, PACK, J], F32, name="picked")
+        u_rows = keep.tile([P, PACK, J], BF16, name="u_rows", align_bytes=64)
+        pieces = [(t, 0, J) for t in range(PACK - 1)] + [(PACK - 1, h * HALF, (h + 1) * HALF) for h in range(halves)]
+        for t, j0, j1 in pieces:
+            nc.scalar.activation(picked[:, t, j0:j1], x_sb[t][:].indirect(list_x[:, j0 // 16 : j1 // 16]), ACT.Copy)
+            nc.vector.scalar_tensor_tensor(
+                u_rows[:, t, j0:j1], picked[:, t, j0:j1], fk_sb[:, t : t + 1], centre[:, t, j0:j1],
+                ALU.mult, ALU.subtract,
+            )
+        u_grouped = keep.tile([P, J * PACK], BF16, name="u_grouped", align_bytes=64)
+        u_codes = keep.tile([P, J], U32, name="u_codes", align_bytes=64)
+        u_scales = keep.tile([P, J], U8, name="u_scales", align_bytes=64)
+        for h in range(halves):
+            nc.vector.tensor_copy(
+                u_grouped[:, h * HALF * PACK : (h + 1) * HALF * PACK].rearrange("p (c i t) -> p c t i", t=PACK, i=4),
+                u_rows[:, :, h * HALF : (h + 1) * HALF].rearrange("p t (c i) -> p c t i", i=4),
+            )
+        for h in range(halves):
+            nc.vector.quantize_mx(
+                out=u_codes[:, h * HALF : (h + 1) * HALF].bitcast(E5M2),
+                scales=u_scales[:, h * HALF : (h + 1) * HALF],
+                in_=u_grouped[:, h * HALF * PACK : (h + 1) * HALF * PACK],
+            )
+
+        xo_g = keep.tile([P, J], U32, name="xo_g", align_bytes=64)
+        for h in range(halves):
+            nc.vector.tensor_copy(
+                xo_g[:, h * HALF : (h + 1) * HALF],
+                xo_raw[:].bitcast(U32).indirect(list_o[:, h * HALF // 16 : (h + 1) * HALF // 16]),
+            )
+        w2_sb = keep.tile([P, R], I32, name="w2_sb", align_bytes=64)
+        w_sb = keep.tile([P, R], I32, name="w_sb", align_bytes=64)
+        for dst, raw in ((w_sb, w_raw), (w2_sb, w2_raw)):
+            nc.scalar.copy(
+                dst[:].bitcast(U32).rearrange("p (t c i) -> p c t i", t=PACK, i=4),
+                raw[:].bitcast(U32).rearrange("p (c i t) -> p c t i", t=PACK, i=4),
+            )
+
+        acc = [psum.tile([P, PACK, HALF], F32, name="acc_%d" % h) for h in range(halves)]
+        for h in range(halves):
+            js = slice(h * HALF, (h + 1) * HALF)
+            for t in range(PACK):
+                nc.tensor.matmul_mx(
+                    out=acc[h][:, t, :],
+                    lhsT=w_sb[:, t * P : (t + 1) * P].bitcast(E5M2),
+                    lhsT_scale=planes[:, W0 + t * P : W0 + (t + 1) * P],
+                    rhs=u_codes[:, js].bitcast(E5M2),
+                    rhs_scale=u_scales[:, js],
+                    start=(t == 0), stop=False,
+                )
+            for t in range(PACK):
+                nc.tensor.matmul_mx(
+                    out=acc[h][:, t, :],
+                    lhsT=w2_sb[:, t * P : (t + 1) * P].bitcast(E5M2),
+                    lhsT_scale=planes[:, W20 + t * P : W20 + (t + 1) * P],
+                    rhs=xo_g[:, js].bitcast(E4M3),
+                    rhs_scale=planes[:, XO0 + h * HALF : XO0 + (h + 1) * HALF],
+                    start=False, stop=(t == PACK - 1),
+                )
+
+        hid = keep.tile([P, J * PACK], BF16, name="hid", align_bytes=64)
+        h_codes = keep.tile([P, J], U32, name="h_codes", align_bytes=64)
+        h_scales = keep.tile([P, J], U8, name="h_scales", align_bytes=64)
+        for h in range(halves):
+            e0, e1 = h * HALF * PACK, (h + 1) * HALF * PACK
+            sums = acc[h][:].rearrange("p t j -> p j t")
+            nc.scalar.activation(
+                lagged[:, LAG * PACK + e0 : LAG * PACK + e1].rearrange("p (j t) -> p j t", t=PACK),
+                sums, ACT.Relu, scale=0.5,
+            )
+            nc.vector.scalar_tensor_tensor(
+                hid[:, e0:e1].rearrange("p (j t) -> p j t", t=PACK), sums, 0.0,
+                lagged[:, e0:e1].rearrange("p (j t) -> p j t", t=PACK), ALU.max, ALU.subtract,
+            )
+        prod = [psum.tile([P, N], F32, name="prod_%d" % h) for h in range(halves)]
+        for h in range(halves):
+            js = slice(h * HALF, (h + 1) * HALF)
+            nc.vector.quantize_mx(
+                out=h_codes[:, js].bitcast(E5M2), scales=h_scales[:, js],
+                in_=hid[:, h * HALF * PACK : (h + 1) * HALF * PACK],
+            )
+            nc.tensor.matmul_mx(
+                out=prod[h][:], lhsT=h_codes[:, js].bitcast(E5M2), lhsT_scale=h_scales[:, js],
+                rhs=wb_sb[:].bitcast(E4M3), rhs_scale=planes[:, WB0 : WB0 + N], start=True, stop=True,
+            )
+
+        rs_part = keep.tile([P, halves, N], F32, name="rs_part")
+        nc.scalar.activation(rs_part[:], rs_sb[:], ACT.Copy, scale=0.3)
+        size = keep.tile([P, halves, N], F32, name="size")
+        shifted = keep.tile([P, halves, N], F32, name="shifted")
+        y = keep.tile([P, halves, N], F32, name="y")
+        for h in range(halves):
+            denom = keep.tile([P, 1], F32, name="denom_%d" % h)
+            inv = keep.tile([P, 1], F32, name="inv_%d" % h)
+            nc.scalar.activation(size[:, h, :], prod[h][:], ACT.Abs)
+            nc.vector.tensor_scalar(shifted[:, h, :], size[:, h, :], 0.2, None, ALU.add, ALU.max, accum_out=denom[:])
+            nc.vector.reciprocal(inv[:], denom[:])
+            nc.vector.scalar_tensor_tensor(y[:, h, :], prod[h][:], inv[:], rs_part[:, h, :], ALU.mult, ALU.add)
+            nc.sync.dma_start(out[h * HALF : (h + 1) * HALF, :], y[:, h, :])

@@ -20,6 +20,7 @@ P = 128
 PACK = 4
 HALF = 128
 LAG = 2
+CHUNK = 64
 
 
 def tile_list_sum_offsetpicks_othertable_lagged_rowpeaks_kernel(
@@ -45,20 +46,18 @@ def tile_list_sum_offsetpicks_othertable_lagged_rowpeaks_kernel(
         nc.scalar.dma_start(fk_sb[:], fk.rearrange("(p t) o -> p (t o)", t=PACK))
         ws_raw = keep.tile([P, 2, R], U8, name="ws_raw", align_bytes=64)
         xs_raw = keep.tile([P, Z], U8, name="xs_raw", align_bytes=64)
-        planes = keep.tile([P, 2 * R + J + N], U8, name="planes", align_bytes=64)
-        W0, W20, XO0, WB0 = 0, R, 2 * R, 2 * R + J
+        planes = keep.tile([P, 2 * R + J], U8, name="planes", align_bytes=64)
+        W0, W20, XO0 = 0, R, 2 * R
         nc.vector.memset(xs_raw[:].bitcast(I32), 0)
         nc.vector.memset(ws_raw[:].rearrange("p a c -> p (a c)").bitcast(I32), 0)
-        nc.gpsimd.memset(planes[:, WB0 : WB0 + N].bitcast(I32), 0)
         nc.scalar.dma_start(xs_raw[0:16, :].bitcast(I32), xo_scales[0].bitcast(I32))
         nc.scalar.dma_start(ws_raw[0:16, 0, :].bitcast(I32), w_scales[0].bitcast(I32))
         nc.scalar.dma_start(ws_raw[0:16, 1, :].bitcast(I32), w2_scales[0].bitcast(I32))
-        nc.gpsimd.dma_start(planes[0:16, WB0 : WB0 + N].bitcast(I32), wb_scales[0].bitcast(I32))
 
         lagged = keep.tile([P, (LAG + J) * PACK], F32, name="lagged")
         before_first = keep.tile([P, LAG * PACK], F32, name="before_first")
         nc.vector.memset(before_first[:], 0.0)
-        nc.scalar.activation(lagged[:, 0 : LAG * PACK], before_first[:], ACT.Relu, scale=0.5)
+        nc.scalar.activation(lagged[:, 0 : LAG * PACK], before_first[:], ACT.Relu)
 
         ow_sb = keep.tile([P, PACK, J], F32, name="ow_sb")
         nc.sync.dma_start(ow_sb[:], ow.rearrange("(p t) j -> p t j", t=PACK))
@@ -68,13 +67,6 @@ def tile_list_sum_offsetpicks_othertable_lagged_rowpeaks_kernel(
             x_t = keep.tile([P, T], F32, name="x_%d" % t)
             nc.sync.dma_start(x_t[:], x_rows[:, t, :])
             x_sb.append(x_t)
-        xo_raw = keep.tile([P, Z], I32, name="xo_raw", align_bytes=64)
-        w2_raw = keep.tile([P, R], I32, name="w2_raw", align_bytes=64)
-        w_raw = keep.tile([P, R], I32, name="w_raw", align_bytes=64)
-        nc.sync.dma_start(w_raw[:], words(w_words))
-        nc.sync.dma_start(w2_raw[:], words(w2_words))
-        nc.sync.dma_start(xo_raw[:], words(xo_words))
-
         xs_g = keep.tile([P, J], U8, name="xs_g", align_bytes=64)
         nc.vector.tensor_copy(xs_g[:], xs_raw[:].indirect(list_o[:]))
         for a in range(2):
@@ -83,18 +75,34 @@ def tile_list_sum_offsetpicks_othertable_lagged_rowpeaks_kernel(
                 ws_raw[:, a, :].rearrange("p (c i t) -> p c t i", t=PACK, i=16),
             )
         nc.vector.tensor_copy(planes[:, XO0 : XO0 + J].bitcast(I32), xs_g[:].bitcast(I32))
+
+        xo_raw = keep.tile([P, Z], I32, name="xo_raw", align_bytes=64)
+        w2_raw = keep.tile([P, R], I32, name="w2_raw", align_bytes=64)
+        w_raw = keep.tile([P, R], I32, name="w_raw", align_bytes=64)
+        nc.sync.dma_start(w_raw[:], words(w_words))
+        nc.sync.dma_start(w2_raw[:], words(w2_words))
         for q in range(1, 4):
             nc.sync.dma_start(
                 planes[32 * q : 32 * q + 4, :].bitcast(I32), planes[4 * q : 4 * q + 4, :].bitcast(I32)
             )
+        nc.sync.dma_start(xo_raw[:], words(xo_words))
 
         wb_sb = keep.tile([P, N], I32, name="wb_sb", align_bytes=64)
-        nc.sync.dma_start(wb_sb[:], words(wb_words))
         rs_sb = keep.tile([P, halves, N], F32, name="rs_sb")
         nc.sync.dma_start(rs_sb[:], rs.rearrange("(h p) n -> p h n", p=P))
 
+        nc.sync.dma_start(wb_sb[:], words(wb_words))
+        wb_plane = keep.tile([P, N], U8, name="wb_plane", align_bytes=64)
+        nc.gpsimd.memset(wb_plane[:].bitcast(I32), 0)
+        for q in range(4):
+            nc.sync.dma_start(
+                wb_plane[32 * q : 32 * q + 4, :].bitcast(I32), wb_scales[0, 4 * q : 4 * q + 4, :].bitcast(I32)
+            )
+
         centre = keep.tile([P, PACK, J], F32, name="centre")
-        for t in range(PACK):
+        for t in range(PACK // 2):
+            nc.scalar.activation(centre[:, t, :], ow_sb[:, t, :], ACT.Copy, scale=fk_sb[:, t : t + 1])
+        for t in range(PACK // 2, PACK):
             nc.vector.tensor_scalar(centre[:, t, :], ow_sb[:, t, :], fk_sb[:, t : t + 1], None, ALU.mult)
         picked = keep.tile([P, PACK, J], F32, name="picked")
         u_rows = keep.tile([P, PACK, J], BF16, name="u_rows", align_bytes=64)
@@ -159,16 +167,15 @@ def tile_list_sum_offsetpicks_othertable_lagged_rowpeaks_kernel(
         hid = keep.tile([P, J * PACK], BF16, name="hid", align_bytes=64)
         h_codes = keep.tile([P, J], U32, name="h_codes", align_bytes=64)
         h_scales = keep.tile([P, J], U8, name="h_scales", align_bytes=64)
-        for h in range(halves):
-            e0, e1 = h * HALF * PACK, (h + 1) * HALF * PACK
-            sums = acc[h][:].rearrange("p t j -> p j t")
+        for j0 in range(0, J, CHUNK):
+            e0, e1 = j0 * PACK, (j0 + CHUNK) * PACK
+            c0 = j0 % HALF
             nc.scalar.activation(
                 lagged[:, LAG * PACK + e0 : LAG * PACK + e1].rearrange("p (j t) -> p j t", t=PACK),
-                sums, ACT.Relu, scale=0.5,
+                acc[j0 // HALF][:, :, c0 : c0 + CHUNK].rearrange("p t j -> p j t"), ACT.Relu,
             )
             nc.vector.scalar_tensor_tensor(
-                hid[:, e0:e1].rearrange("p (j t) -> p j t", t=PACK), sums, 0.0,
-                lagged[:, e0:e1].rearrange("p (j t) -> p j t", t=PACK), ALU.max, ALU.subtract,
+                hid[:, e0:e1], lagged[:, e0:e1], -0.5, lagged[:, LAG * PACK + e0 : LAG * PACK + e1], ALU.mult, ALU.add,
             )
         prod = [psum.tile([P, N], F32, name="prod_%d" % h) for h in range(halves)]
         for h in range(halves):
@@ -179,11 +186,11 @@ def tile_list_sum_offsetpicks_othertable_lagged_rowpeaks_kernel(
             )
             nc.tensor.matmul_mx(
                 out=prod[h][:], lhsT=h_codes[:, js].bitcast(E5M2), lhsT_scale=h_scales[:, js],
-                rhs=wb_sb[:].bitcast(E4M3), rhs_scale=planes[:, WB0 : WB0 + N], start=True, stop=True,
+                rhs=wb_sb[:].bitcast(E4M3), rhs_scale=wb_plane[:], start=True, stop=True,
             )
 
         rs_part = keep.tile([P, halves, N], F32, name="rs_part")
-        nc.scalar.activation(rs_part[:], rs_sb[:], ACT.Copy, scale=0.3)
+        nc.vector.tensor_scalar(rs_part[:], rs_sb[:], 0.3, None, ALU.mult)
         size = keep.tile([P, halves, N], F32, name="size")
         shifted = keep.tile([P, halves, N], F32, name="shifted")
         y = keep.tile([P, halves, N], F32, name="y")

from contextlib import ExitStack

import concourse.mybir as mybir

K, T, J, R, F, Z, N = 512, 512, 256, 512, 512, 1024, 256
FLOPS = 2 * K * R * J + 2 * F * R * J + 2 * R * J * N

F32 = mybir.dt.float32
BF16 = mybir.dt.bfloat16
I32 = mybir.dt.int32
U32 = mybir.dt.uint32
U16 = mybir.dt.uint16
U8 = mybir.dt.uint8
E4M3 = mybir.dt.float8_e4m3fn_x4
E5M2 = mybir.dt.float8_e5m2_x4
ALU = mybir.AluOpType
ACT = mybir.ActivationFunctionType

P = 128
PACK = 4
HALF = 128
LAG = 2
CHUNK = 64


def tile_list_sum_offsetpicks_othertable_lagged_rowpeaks_kernel(
    tc, xf, ow, fk, w_words, w_scales, xo_words, xo_scales, w2_words, w2_scales,
    wb_words, wb_scales, rs, offs, offs2, out,
):
    nc = tc.nc
    halves = J // HALF

    def words(ap):
        return ap[0].rearrange("p n t -> p (n t)").bitcast(I32)

    with ExitStack() as ctx:
        keep = ctx.enter_context(tc.tile_pool(name="keep", bufs=1))
        psum = ctx.enter_context(tc.psum_pool(name="psum", bufs=1))

        list_x = keep.tile([P, J // 16], U16, name="list_x")
        list_o = keep.tile([P, J // 16], U16, name="list_o")
        nc.sync.dma_start(list_o[:], offs2)
        nc.sync.dma_start(list_x[:], offs)

        fk_sb = keep.tile([P, PACK], F32, name="fk_sb")
        nc.scalar.dma_start(fk_sb[:], fk.rearrange("(p t) o -> p (t o)", t=PACK))
        ws_raw = keep.tile([P, 2, R], U8, name="ws_raw", align_bytes=64)
        xs_raw = keep.tile([P, Z], U8, name="xs_raw", align_bytes=64)
        planes = keep.tile([P, 2 * R + J], U8, name="planes", align_bytes=64)
        W0, W20, XO0 = 0, R, 2 * R
        nc.vector.memset(xs_raw[:].bitcast(I32), 0)
        nc.vector.memset(ws_raw[:].rearrange("p a c -> p (a c)").bitcast(I32), 0)
        nc.scalar.dma_start(xs_raw[0:16, :].bitcast(I32), xo_scales[0].bitcast(I32))
        nc.scalar.dma_start(ws_raw[0:16, 0, :].bitcast(I32), w_scales[0].bitcast(I32))
        nc.scalar.dma_start(ws_raw[0:16, 1, :].bitcast(I32), w2_scales[0].bitcast(I32))

        lagged = keep.tile([P, (LAG + J) * PACK], F32, name="lagged")
        before_first = keep.tile([P, LAG * PACK], F32, name="before_first")
        nc.vector.memset(before_first[:], 0.0)
        nc.scalar.activation(lagged[:, 0 : LAG * PACK], before_first[:], ACT.Relu)

        ow_sb = keep.tile([P, PACK, J], F32, name="ow_sb")
        nc.sync.dma_start(ow_sb[:], ow.rearrange("(p t) j -> p t j", t=PACK))
        x_rows = xf.rearrange("(p t) c -> p t c", t=PACK)
        x_sb = []
        for t in range(PACK):
            x_t = keep.tile([P, T], F32, name="x_%d" % t)
            nc.sync.dma_start(x_t[:], x_rows[:, t, :])
            x_sb.append(x_t)
        xs_g = keep.tile([P, J], U8, name="xs_g", align_bytes=64)
        nc.vector.tensor_copy(xs_g[:], xs_raw[:].indirect(list_o[:]))
        for a in range(2):
            nc.vector.tensor_copy(
                planes[:, a * R : (a + 1) * R].rearrange("p (t c i) -> p c t i", t=PACK, i=16),
                ws_raw[:, a, :].rearrange("p (c i t) -> p c t i", t=PACK, i=16),
            )
        nc.vector.tensor_copy(planes[:, XO0 : XO0 + J].bitcast(I32), xs_g[:].bitcast(I32))

        xo_raw = keep.tile([P, Z], I32, name="xo_raw", align_bytes=64)
        w2_raw = keep.tile([P, R], I32, name="w2_raw", align_bytes=64)
        w_raw = keep.tile([P, R], I32, name="w_raw", align_bytes=64)
        nc.sync.dma_start(w_raw[:], words(w_words))
        nc.sync.dma_start(w2_raw[:], words(w2_words))
        for q in range(1, 4):
            nc.sync.dma_start(
                planes[32 * q : 32 * q + 4, :].bitcast(I32), planes[4 * q : 4 * q + 4, :].bitcast(I32)
            )
        nc.sync.dma_start(xo_raw[:], words(xo_words))

        wb_sb = keep.tile([P, N], I32, name="wb_sb", align_bytes=64)
        rs_sb = keep.tile([P, halves, N], F32, name="rs_sb")
        nc.sync.dma_start(rs_sb[:], rs.rearrange("(h p) n -> p h n", p=P))

        nc.sync.dma_start(wb_sb[:], words(wb_words))
        wb_plane = keep.tile([P, N], U8, name="wb_plane", align_bytes=64)
        nc.gpsimd.memset(wb_plane[:].bitcast(I32), 0)
        for q in range(4):
            nc.sync.dma_start(
                wb_plane[32 * q : 32 * q + 4, :].bitcast(I32), wb_scales[0, 4 * q : 4 * q + 4, :].bitcast(I32)
            )

        centre = keep.tile([P, PACK, J], F32, name="centre")
        for t in range(PACK // 2):
            nc.scalar.activation(centre[:, t, :], ow_sb[:, t, :], ACT.Copy, scale=fk_sb[:, t : t + 1])
        for t in range(PACK // 2, PACK):
            nc.vector.tensor_scalar(centre[:, t, :], ow_sb[:, t, :], fk_sb[:, t : t + 1], None, ALU.mult)
        picked = keep.tile([P, PACK, J], F32, name="picked")
        u_rows = keep.tile([P, PACK, J], BF16, name="u_rows", align_bytes=64)
        pieces = [(t, 0, J) for t in range(PACK - 1)] + [(PACK - 1, h * HALF, (h + 1) * HALF) for h in range(halves)]
        for t, j0, j1 in pieces:
            nc.scalar.activation(picked[:, t, j0:j1], x_sb[t][:].indirect(list_x[:, j0 // 16 : j1 // 16]), ACT.Copy)
            nc.vector.scalar_tensor_tensor(
                u_rows[:, t, j0:j1], picked[:, t, j0:j1], fk_sb[:, t : t + 1], centre[:, t, j0:j1],
                ALU.mult, ALU.subtract,
            )
        u_grouped = keep.tile([P, J * PACK], BF16, name="u_grouped", align_bytes=64)
        u_codes = keep.tile([P, J], U32, name="u_codes", align_bytes=64)
        u_scales = keep.tile([P, J], U8, name="u_scales", align_bytes=64)
        for h in range(halves):
            nc.vector.tensor_copy(
                u_grouped[:, h * HALF * PACK : (h + 1) * HALF * PACK].rearrange("p (c i t) -> p c t i", t=PACK, i=4),
                u_rows[:, :, h * HALF : (h + 1) * HALF].rearrange("p t (c i) -> p c t i", i=4),
            )
        for h in range(halves):
            nc.vector.quantize_mx(
                out=u_codes[:, h * HALF : (h + 1) * HALF].bitcast(E5M2),
                scales=u_scales[:, h * HALF : (h + 1) * HALF],
                in_=u_grouped[:, h * HALF * PACK : (h + 1) * HALF * PACK],
            )

        xo_g = keep.tile([P, J], U32, name="xo_g", align_bytes=64)
        for h in range(halves):
            nc.vector.tensor_copy(
                xo_g[:, h * HALF : (h + 1) * HALF],
                xo_raw[:].bitcast(U32).indirect(list_o[:, h * HALF // 16 : (h + 1) * HALF // 16]),
            )
        w2_sb = keep.tile([P, R], I32, name="w2_sb", align_bytes=64)
        w_sb = keep.tile([P, R], I32, name="w_sb", align_bytes=64)
        for dst, raw in ((w_sb, w_raw), (w2_sb, w2_raw)):
            nc.scalar.copy(
                dst[:].bitcast(U32).rearrange("p (t c i) -> p c t i", t=PACK, i=4),
                raw[:].bitcast(U32).rearrange("p (c i t) -> p c t i", t=PACK, i=4),
            )

        acc = [psum.tile([P, PACK, HALF], F32, name="acc_%d" % h) for h in range(halves)]
        for h in range(halves):
            js = slice(h * HALF, (h + 1) * HALF)
            for t in range(PACK):
                nc.tensor.matmul_mx(
                    out=acc[h][:, t, :],
                    lhsT=w_sb[:, t * P : (t + 1) * P].bitcast(E5M2),
                    lhsT_scale=planes[:, W0 + t * P : W0 + (t + 1) * P],
                    rhs=u_codes[:, js].bitcast(E5M2),
                    rhs_scale=u_scales[:, js],
                    start=(t == 0), stop=False,
                )
            for t in range(PACK):
                nc.tensor.matmul_mx(
                    out=acc[h][:, t, :],
                    lhsT=w2_sb[:, t * P : (t + 1) * P].bitcast(E5M2),
                    lhsT_scale=planes[:, W20 + t * P : W20 + (t + 1) * P],
                    rhs=xo_g[:, js].bitcast(E4M3),
                    rhs_scale=planes[:, XO0 + h * HALF : XO0 + (h + 1) * HALF],
                    start=False, stop=(t == PACK - 1),
                )

        hid = keep.tile([P, J * PACK], BF16, name="hid", align_bytes=64)
        h_codes = keep.tile([P, J], U32, name="h_codes", align_bytes=64)
        h_scales = keep.tile([P, J], U8, name="h_scales", align_bytes=64)
        for j0 in range(0, J, CHUNK):
            e0, e1 = j0 * PACK, (j0 + CHUNK) * PACK
            c0 = j0 % HALF
            nc.scalar.activation(
                lagged[:, LAG * PACK + e0 : LAG * PACK + e1].rearrange("p (j t) -> p j t", t=PACK),
                acc[j0 // HALF][:, :, c0 : c0 + CHUNK].rearrange("p t j -> p j t"), ACT.Relu,
            )
            nc.vector.scalar_tensor_tensor(
                hid[:, e0:e1], lagged[:, e0:e1], -0.5, lagged[:, LAG * PACK + e0 : LAG * PACK + e1], ALU.mult, ALU.add,
            )
        prod = [psum.tile([P, N], F32, name="prod_%d" % h) for h in range(halves)]
        for h in range(halves):
            js = slice(h * HALF, (h + 1) * HALF)
            nc.vector.quantize_mx(
                out=h_codes[:, js].bitcast(E5M2), scales=h_scales[:, js],
                in_=hid[:, h * HALF * PACK : (h + 1) * HALF * PACK],
            )
            nc.tensor.matmul_mx(
                out=prod[h][:], lhsT=h_codes[:, js].bitcast(E5M2), lhsT_scale=h_scales[:, js],
                rhs=wb_sb[:].bitcast(E4M3), rhs_scale=wb_plane[:], start=True, stop=True,
            )

        rs_part = keep.tile([P, halves, N], F32, name="rs_part")
        nc.vector.tensor_scalar(rs_part[:], rs_sb[:], 0.3, None, ALU.mult)
        size = keep.tile([P, halves, N], F32, name="size")
        shifted = keep.tile([P, halves, N], F32, name="shifted")
        y = keep.tile([P, halves, N], F32, name="y")
        for h in range(halves):
            denom = keep.tile([P, 1], F32, name="denom_%d" % h)
            inv = keep.tile([P, 1], F32, name="inv_%d" % h)
            nc.scalar.activation(size[:, h, :], prod[h][:], ACT.Abs)
            nc.vector.tensor_scalar(shifted[:, h, :], size[:, h, :], 0.2, None, ALU.add, ALU.max, accum_out=denom[:])
            nc.vector.reciprocal(inv[:], denom[:])
            nc.vector.scalar_tensor_tensor(y[:, h, :], prod[h][:], inv[:], rs_part[:, h, :], ALU.mult, ALU.add)
            nc.sync.dma_start(out[h * HALF : (h + 1) * HALF, :], y[:, h, :])
